import numpy as np
import ml_dtypes


def mxq(x, axis, fmt="e4m3"):
    dtype, down = {"e4m3": (ml_dtypes.float8_e4m3fn, 7), "e5m2": (ml_dtypes.float8_e5m2, 14)}[fmt]
    v = np.moveaxis(np.asarray(x, np.float32).astype(ml_dtypes.bfloat16).astype(np.float64), axis, -1)
    blocks = v.reshape(v.shape[:-1] + (-1, 32))
    amax = np.abs(blocks).max(-1, keepdims=True)
    byte = np.maximum(np.where(amax > 0, np.frexp(amax)[1] - 1 + 127, 0) - down, 1)
    scale = np.exp2(byte - 127.0)
    codes = (blocks / scale).astype(np.float32).astype(dtype).astype(np.float64)
    return np.moveaxis((codes * scale).reshape(v.shape), -1, axis)


WIDE = False


def mx_kscale(k):
    if not WIDE:
        return np.ones(k)
    levels = np.array([10, -10, 5, -5, 0])
    if k % 512:
        return np.exp2(np.random.permutation(np.resize(levels, k // 32))).repeat(32)
    a = np.empty((k // 512, 16))
    for p in range(k // 512):
        a[p, :8] = np.random.permutation(np.resize(levels, 8))
        for g in range(8):
            far = levels[np.abs(levels - a[p, g]) >= 10]
            a[p, g + 8] = far[np.random.randint(len(far))]
    return np.exp2(a.ravel()).repeat(32)


BF16 = ml_dtypes.bfloat16


def bf(x):
    return np.asarray(x, np.float32).astype(BF16)


def f64(x):
    return np.asarray(x).astype(np.float64)


E2M1 = np.array([0.0, 0.5, 1.0, 1.5, 2.0, 3.0, 4.0, 6.0, -0.0, -0.5, -1.0, -1.5, -2.0, -3.0, -4.0, -6.0])


def pack_weight(w, fmt):
    k, n = w.shape
    w = f64(bf(w)).reshape(k // 32, 32, n)
    amax = np.abs(w).max(1)
    if fmt == "e4m3":
        byte = np.frexp(amax)[1] - 1 + 127 - 7
    else:
        mant, ex = np.frexp(amax / 6.0)
        byte = np.where(mant > 0.5, ex, ex - 1) + 127
    byte = np.clip(np.where(amax > 0, byte, 1), 1, 254)
    scaled = (w * np.exp2(127.0 - byte)[:, None, :]).reshape(k, n).astype(np.float32)
    by_word = np.ascontiguousarray(scaled.reshape(k // 512, 128, 4, n).transpose(0, 1, 3, 2))
    if fmt == "e4m3":
        words = by_word.astype(ml_dtypes.float8_e4m3fn).view(np.uint8)
    else:
        c = by_word.astype(ml_dtypes.float4_e2m1fn).view(np.uint8) & 0xF
        words = c[..., 0::2] | (c[..., 1::2] << 4)
    return np.ascontiguousarray(words), np.ascontiguousarray(byte.astype(np.uint8).reshape(k // 512, 16, n))


def unpack_weight(words, scales, fmt):
    g, p, n, _ = words.shape
    if fmt == "e4m3":
        vals = np.ascontiguousarray(words).view(ml_dtypes.float8_e4m3fn).astype(np.float64)
    else:
        nib = np.empty((g, p, n, 4), np.uint8)
        nib[..., 0::2] = words & 0xF
        nib[..., 1::2] = words >> 4
        vals = E2M1[nib]
    vals = vals * np.repeat(np.exp2(scales.astype(np.float64) - 127.0), 8, axis=1)[..., None]
    return vals.transpose(0, 1, 3, 2).reshape(g * 512, n)
def pack4(w):
    words, scales = pack_weight(w, "e2m1")
    return words.reshape(words.shape[0], 128, -1), scales


def unpack4(words, scales):
    return unpack_weight(words.reshape(words.shape[0], 128, -1, 2), scales, "e2m1")


M, K, P = 2048, 512, 1024


def setup_inputs():
    s, t = mx_kscale(K), mx_kscale(P)
    reach = np.random.uniform(0.5, 1.3, M)
    a = np.random.standard_normal((K, M)) * reach * s[:, None]
    b = np.random.standard_normal((K, P)) / np.sqrt(K) / s[:, None] * t
    a_words, a_scales = pack4(a)
    b_words, b_scales = pack4(b)
    return {"a_words": a_words, "a_scales": a_scales,
            "b_words": b_words, "b_scales": b_scales,
            "mu": bf(0.3 * np.random.standard_normal(P) * t),
            "r": bf(0.5 * np.random.standard_normal((P, P)) / np.sqrt(P) / t[:, None]),
            "e": bf(np.random.uniform(-1.7, 1.7, M))}


def reference(a_words, a_scales, b_words, b_scales, mu, r, e):
    a = unpack4(a_words, a_scales)
    b = unpack4(b_words, b_scales)
    x = (a.T @ b) - f64(mu)
    z = mxq(x, 1, "e4m3") @ mxq(f64(r), 0, "e4m3")
    z2 = np.square(z)
    h = z2.mean(axis=1)
    g = np.square(f64(e) / (1.0 - h))
    c = z2 * g[:, None]
    return c, c.mean(axis=1)

@@ -1,0 +1,315 @@
+from contextlib import ExitStack
+
+import concourse.mybir as mybir
+from concourse.masks import make_identity
+
+M, K, P = 2048, 512, 1024
+FLOPS = 2 * M * K * P + 2 * M * P * P
+
+F32 = mybir.dt.float32
+BF16 = mybir.dt.bfloat16
+U32 = mybir.dt.uint32
+I32 = mybir.dt.int32
+U8 = mybir.dt.uint8
+FP8X4 = mybir.dt.float8_e4m3fn_x4
+FP4X4 = mybir.dt.float4_e2m1fn_x4
+MULT = mybir.AluOpType.mult
+ADD = mybir.AluOpType.add
+IDENTITY = mybir.ActivationFunctionType.Identity
+SQUARE = mybir.ActivationFunctionType.Square
+COPY = mybir.ActivationFunctionType.Copy
+
+LANES = 128
+PACK = 4
+GROUPS = P // 512
+CHUNK = 512
+CHUNKS = M // CHUNK
+TILES = M // LANES
+GROUPS_OF_TILES = [[2 * i, 2 * i + 1] for i in range(7)] + [[14], [15]]
+ON_VECTOR = {3: (1, 3, 5)}
+ORDER = "R0 B R1 R2 A00 R3 R4 A01 X0 A10 R5 E R6 R7 A11 X1 P0 X2 G0 A20 P1 A21 X3 G1 P2 A30 P3 X4 G2 X5 G3 A31 P4 X6 G4 P5 P6 X7 P7 G5 P8 G6 G7 G8"
+
+
+def tile_ridge_cook_distances_s4_kernel(tc, a_words, a_scales, b_words, b_scales, mu, r, e, out_0, out_1):
+    nc = tc.nc
+    with ExitStack() as ctx:
+        keep = ctx.enter_context(tc.tile_pool(name="keep", bufs=1))
+        ring = ctx.enter_context(tc.tile_pool(name="ring", bufs=4))
+        rows_pool = ctx.enter_context(tc.tile_pool(name="rows", bufs=8))
+        outs = ctx.enter_context(tc.tile_pool(name="outs", bufs=8))
+        psum = ctx.enter_context(tc.psum_pool(name="psum", bufs=4))
+        ctx.enter_context(tc.manual_schedule())
+
+        vec_rows = keep.tile([LANES, LANES], BF16)
+        e_rows = keep.tile([LANES, LANES], BF16)
+        b_plane_raw = keep.tile([LANES, P], U8, align_bytes=64)
+        a_plane = keep.tile([LANES, M], U8, align_bytes=64)
+        b_raw = keep.tile([LANES, 2 * P], U8, align_bytes=64)
+        b_codes = keep.tile([LANES, 2 * P], U8, align_bytes=64)
+        b_plane = keep.tile([LANES, P], U8, align_bytes=64)
+        a_codes = keep.tile([LANES, 2 * M], U8, align_bytes=64)
+        r_raw = keep.tile([LANES, GROUPS, PACK, P], BF16, align_bytes=64)
+        r_codes = keep.tile([LANES, GROUPS, P], U32, align_bytes=64)
+        r_plane = keep.tile([LANES, GROUPS, P], U8, align_bytes=64)
+        x_codes = keep.tile([LANES, CHUNKS, GROUPS, CHUNK], U32, align_bytes=64)
+        x_plane = keep.tile([LANES, CHUNKS, GROUPS, CHUNK], U8, align_bytes=64)
+        neg_mu = keep.tile([LANES, GROUPS * PACK], F32)
+        e_col = keep.tile([LANES, TILES], F32)
+        d_cols = keep.tile([LANES, LANES], F32)
+        ident = keep.tile([LANES, LANES], BF16)
+        ident_f = keep.tile([LANES, LANES], F32)
+        warm = keep.tile([LANES, 1], F32)
+
+        nc.vector.memset(a_plane[:].bitcast(I32), 0)
+        nc.gpsimd.memset(b_plane_raw[:].bitcast(I32), 0)
+        nc.vector.memset(vec_rows[:], 0.0)
+        nc.vector.memset(warm[:], 0.0)
+        nc.vector.memset(e_rows[:], 0.0)
+        for quad in range(4):
+            nc.gpsimd.dma_start(
+                out=b_plane_raw[32 * quad : 32 * quad + 4, :].bitcast(I32),
+                in_=b_scales[0, 4 * quad : 4 * quad + 4, :].bitcast(I32),
+            )
+        make_identity(nc, ident[:])
+
+        def load_a(c):
+            cols = slice(2 * CHUNK * c, 2 * CHUNK * (c + 1))
+            nc.sync.dma_start(out=a_codes[:, cols].bitcast(I32), in_=a_words[0][:, cols].bitcast(I32))
+
+        def load_a_scales(quads):
+            for quad in quads:
+                nc.sync.dma_start(
+                    out=a_plane[32 * quad : 32 * quad + 4, :].bitcast(I32),
+                    in_=a_scales[0, 4 * quad : 4 * quad + 4, :].bitcast(I32),
+                )
+
+        def load_r(g, half):
+            rows = r[512 * g : 512 * (g + 1), :].rearrange("(q t i) c -> t q i c", q=16, t=4)
+            cols = slice(512 * half, 512 * (half + 1))
+            for t in range(PACK):
+                nc.sync.dma_start(out=r_raw[:, g, t, cols], in_=rows[t][:, :, cols])
+
+        nc.sync.dma_start(out=b_raw[:].bitcast(I32), in_=b_words[0].bitcast(I32))
+        load_a(0)
+        load_a_scales((0, 1))
+        load_r(0, 0)
+        load_a_scales((2, 3))
+        nc.sync.dma_start(out=vec_rows[0:4, :], in_=mu[0:512].rearrange("(q t i) -> t q i", q=16, t=4))
+        nc.sync.dma_start(out=vec_rows[4:8, :], in_=mu[512:1024].rearrange("(q t i) -> t q i", q=16, t=4))
+        load_r(0, 1)
+        load_a(1)
+        load_r(1, 0)
+        load_r(1, 1)
+        load_a(2)
+        load_a(3)
+        nc.sync.dma_start(out=e_rows[0:TILES, :], in_=e.rearrange("(t p) -> t p", p=LANES))
+        make_identity(nc, ident_f[:])
+        nc.gpsimd.memset(d_cols[:], 0.0)
+        nc.scalar.activation(out=warm[:], in_=warm[:], func=SQUARE)
+
+        def ready_b():
+            for g in range(GROUPS):
+                nc.vector.tensor_copy(
+                    out=b_plane[:, 512 * g : 512 * (g + 1)].bitcast(I32).rearrange("p (t q w) -> p t q w", t=4, q=16),
+                    in_=b_plane_raw[:, 512 * g : 512 * (g + 1)].bitcast(I32).rearrange("p (q t w) -> p t q w", t=4, q=16),
+                )
+                nc.vector.tensor_copy(
+                    out=b_codes[:, 1024 * g : 1024 * (g + 1)].bitcast(I32).rearrange("p (t q w) -> p t q w", t=4, q=16),
+                    in_=b_raw[:, 1024 * g : 1024 * (g + 1)].bitcast(I32).rearrange("p (q t w) -> p t q w", t=4, q=16),
+                )
+
+            vec_bank = psum.tile([LANES, LANES], BF16, tag="x")
+            nc.tensor.transpose(vec_bank[:], vec_rows[:], ident[:])
+            nc.vector.tensor_scalar(out=neg_mu[:], in0=vec_bank[:, 0 : GROUPS * PACK], scalar1=-1.0, scalar2=None, op0=MULT)
+
+        x_rows = {}
+
+        def stage1(c, g, on_vector):
+            cols = slice(CHUNK * c, CHUNK * (c + 1))
+            if True:
+                rows = rows_pool.tile([LANES, PACK, CHUNK], BF16, tag="rows", name=f"rows_{c}_{g}")
+                x_rows[c, g] = rows
+                for t in range(PACK):
+                    s = PACK * g + t
+                    bank = psum.tile([LANES, CHUNK], F32, tag="x")
+                    nc.tensor.matmul_mx(
+                        out=bank[:],
+                        lhsT=b_codes[:, 256 * s : 256 * (s + 1)].bitcast(FP4X4),
+                        lhsT_scale=b_plane[:, LANES * s : LANES * (s + 1)],
+                        rhs=a_codes[:, 2 * CHUNK * c : 2 * CHUNK * (c + 1)].bitcast(FP4X4),
+                        rhs_scale=a_plane[:, cols],
+                        start=True,
+                        stop=True,
+                    )
+                    if s in on_vector:
+                        nc.vector.tensor_scalar(
+                            out=rows[:, t, :], in0=bank[:], scalar1=neg_mu[:, s : s + 1], scalar2=None, op0=ADD
+                        )
+                    else:
+                        nc.scalar.activation(out=rows[:, t, :], in_=bank[:], func=IDENTITY, bias=neg_mu[:, s : s + 1])
+
+        def interleave(rows, width):
+            grouped = ring.tile([LANES, width, PACK], BF16, tag=f"grouped{width}", align_bytes=64, name="grouped")
+            nc.vector.tensor_copy(
+                out=grouped[:].rearrange("p (c i) t -> p c t i", i=4),
+                in_=rows.rearrange("p t (c i) -> p c t i", i=4),
+            )
+            return grouped
+
+        def quantize(grouped, codes, plane):
+            nc.vector.quantize_mx(
+                out=codes.bitcast(FP8X4), scales=plane, in_=grouped[:].rearrange("p c t -> p (c t)")
+            )
+
+        def quantize_steps(units):
+            made = {}
+            steps = []
+
+            def inter(i):
+                made[i] = interleave(units[i][0], units[i][3])
+
+            def quant(i):
+                quantize(made[i], units[i][1], units[i][2])
+
+            for i in range(0, len(units), 2):
+                steps += [lambda i=i: inter(i), lambda i=i: inter(i + 1)]
+                steps += [lambda i=i: quant(i), lambda i=i: quant(i + 1)]
+            return steps
+
+        def r_units():
+            units = []
+            for g in range(GROUPS):
+                for half in range(2):
+                    cols = slice(512 * half, 512 * (half + 1))
+                    units.append((r_raw[:, g, :, cols], r_codes[:, g, cols], r_plane[:, g, cols], 512))
+            return units
+
+        def x_units(pair):
+            c, cols = pair // 2, slice(256 * (pair % 2), 256 * (pair % 2 + 1))
+            return [(x_rows[c, g][:, :, cols], x_codes[:, c, g, cols], x_plane[:, c, g, cols], 256) for g in range(GROUPS)]
+
+        z2 = {}
+        sums = {}
+
+        def stage2(tiles):
+            sum0 = ring.tile([LANES, len(tiles)], F32, tag="sum0", name="sum0")
+            sum1 = ring.tile([LANES, len(tiles)], F32, tag="sum1", name="sum1")
+            sums[tiles[0]] = (sum0, sum1)
+            for j, tile in enumerate(tiles):
+                c, lo = tile // 4, LANES * (tile % 4)
+                square = outs.tile([LANES, P], F32, tag="square", name="square")
+                z2[tile] = square
+                for half, total in ((0, sum0), (1, sum1)):
+                    cols = slice(512 * half, 512 * (half + 1))
+                    bank = psum.tile([LANES, 512], F32, tag="z")
+                    for g in range(GROUPS):
+                        nc.tensor.matmul_mx(
+                            out=bank[:],
+                            lhsT=x_codes[:, c, g, lo : lo + LANES].bitcast(FP8X4),
+                            lhsT_scale=x_plane[:, c, g, lo : lo + LANES],
+                            rhs=r_codes[:, g, cols].bitcast(FP8X4),
+                            rhs_scale=r_plane[:, g, cols],
+                            start=(g == 0),
+                            stop=(g == GROUPS - 1),
+                        )
+                    nc.scalar.activation(
+                        out=square[:, cols], in_=bank[:], func=SQUARE, accum_out=total[:, j : j + 1]
+                    )
+
+        def finish(tiles):
+            n = len(tiles)
+            sum0, sum1 = sums[tiles[0]]
+            rest = ring.tile([LANES, n], F32, tag="rest", name="rest")
+            inv = ring.tile([LANES, n], F32, tag="inv", name="inv")
+            loo = ring.tile([LANES, n], F32, tag="loo", name="loo")
+            both = ring.tile([LANES, n], F32, tag="both", name="both")
+            d_half = ring.tile([LANES, n], F32, tag="d_half", name="d_half")
+
+            def small1():
+                nc.vector.scalar_tensor_tensor(
+                    out=rest[:], in0=sum0[:], scalar=-1.0 * P, in1=sum1[:], op0=ADD, op1=ADD
+                )
+                nc.gpsimd.tensor_tensor(out=both[:], in0=sum0[:], in1=sum1[:], op=ADD)
+
+            def small2():
+                nc.vector.reciprocal(out=inv[:], in_=rest[:])
+
+            def small3():
+                nc.vector.tensor_tensor(out=loo[:], in0=e_col[:, tiles[0] : tiles[0] + n], in1=inv[:], op=MULT)
+                nc.gpsimd.tensor_tensor(out=d_half[:], in0=both[:], in1=loo[:], op=MULT)
+                nc.gpsimd.tensor_tensor(
+                    out=d_cols[:, tiles[0] : tiles[0] + n], in0=d_half[:], in1=loo[:], op=MULT
+                )
+
+            def scale(j):
+                result = outs.tile([LANES, P], F32, tag="result", name="result")
+                nc.vector.tensor_scalar(
+                    out=result[:], in0=z2[tiles[j]][:], scalar1=loo[:, j : j + 1], scalar2=loo[:, j : j + 1],
+                    op0=MULT, op1=MULT,
+                )
+                nc.sync.dma_start(out=out_0[LANES * tiles[j] : LANES * (tiles[j] + 1), :], in_=result[:])
+
+            return [small1, small2, small3], [lambda j=j: scale(j) for j in range(n)]
+
+        def turn_e():
+            e_bank = psum.tile([LANES, LANES], BF16, tag="x")
+            nc.tensor.transpose(e_bank[:], e_rows[:], ident[:])
+            nc.vector.tensor_scalar(out=e_col[:], in0=e_bank[:, 0:TILES], scalar1=-1.0 * P, scalar2=None, op0=MULT)
+
+        steps = []
+        longs = []
+
+        def add_long(step):
+            longs.append(len(steps))
+            steps.append([step])
+
+        for token in ORDER.split(" "):
+            kind, number = token[0], int(token[1:] or "0")
+            if kind == "A":
+                steps.append([lambda number=number: stage1(number // 10, number % 10, ON_VECTOR.get(number // 10, ()))])
+            elif kind == "P":
+                steps.append([lambda number=number: stage2(GROUPS_OF_TILES[number])])
+            elif kind == "E":
+                steps.append([turn_e])
+            elif kind == "B":
+                steps.append([ready_b])
+            elif kind == "R":
+                add_long(lambda number=number: r_steps(number))
+            elif kind == "X":
+                for i in range(4):
+                    add_long(lambda i=i, number=number: x_steps(number, i))
+            else:
+                for i in range(3):
+                    steps[longs[i - 3]].append(lambda i=i, number=number: short(number, i))
+                for j in range(len(GROUPS_OF_TILES[number])):
+                    add_long(lambda j=j, number=number: scaling(number, j))
+
+        cache = {}
+
+        def r_steps(i):
+            if "r" not in cache:
+                cache["r"] = quantize_steps(r_units())
+            cache["r"][i]()
+
+        def x_steps(c, i):
+            if ("x", c) not in cache:
+                cache["x", c] = quantize_steps(x_units(c))
+            cache["x", c][i]()
+
+        def short(p, i):
+            if ("f", p) not in cache:
+                cache["f", p] = finish(GROUPS_OF_TILES[p])
+            cache["f", p][0][i]()
+
+        def scaling(p, j):
+            cache["f", p][1][j]()
+
+        for group in steps:
+            for step in group:
+                step()
+
+        d_bank = psum.tile([LANES, LANES], F32, tag="x")
+        nc.tensor.transpose(d_bank[:], d_cols[:], ident_f[:])
+        d_rows = keep.tile([TILES, LANES], F32)
+        nc.scalar.activation(out=d_rows[:], in_=d_bank[0:TILES, :], func=COPY, scale=1.0 / P)
+        nc.sync.dma_start(out=out_1.rearrange("(t p) -> t p", p=LANES), in_=d_rows[:])

@@ -26,8 +26,8 @@ CHUNK = 512
 CHUNKS = M // CHUNK
 TILES = M // LANES
 GROUPS_OF_TILES = [[2 * i, 2 * i + 1] for i in range(7)] + [[14], [15]]
-ON_VECTOR = {3: (1, 3, 5)}
-ORDER = "R0 B R1 R2 A00 R3 R4 A01 X0 A10 R5 E R6 R7 A11 X1 P0 X2 G0 A20 P1 A21 X3 G1 P2 A30 P3 X4 G2 X5 G3 A31 P4 X6 G4 P5 P6 X7 P7 G5 P8 G6 G7 G8"
+ON_VECTOR = {0: (1, 3), 3: (3,)}
+ORDER = "B A00 A01 A10 A11 A20 R0 R1 A21 R2 R3 R4 R5 X0 R6 R7 X1 E X2 P0 X3 G0 P1 P2 P3 X4 G1 G2 A30 A31 P4 G3 X5 X6 P5 P6 G4 X7 P7 P8 G5 G6 G7 G8"
 
 
 def tile_ridge_cook_distances_s4_kernel(tc, a_words, a_scales, b_words, b_scales, mu, r, e, out_0, out_1):
@@ -59,28 +59,23 @@ def tile_ridge_cook_distances_s4_kernel(tc, a_words, a_scales, b_words, b_scales
         ident = keep.tile([LANES, LANES], BF16)
         ident_f = keep.tile([LANES, LANES], F32)
         warm = keep.tile([LANES, 1], F32)
+        sum0 = keep.tile([LANES, TILES], F32)
+        sum1 = keep.tile([LANES, TILES], F32)
+        rest = keep.tile([LANES, TILES], F32)
+        inv = keep.tile([LANES, TILES], F32)
+        loo = keep.tile([LANES, TILES], F32)
+        both = keep.tile([LANES, TILES], F32)
+        d_half = keep.tile([LANES, TILES], F32)
 
-        nc.vector.memset(a_plane[:].bitcast(I32), 0)
-        nc.gpsimd.memset(b_plane_raw[:].bitcast(I32), 0)
-        nc.vector.memset(vec_rows[:], 0.0)
-        nc.vector.memset(warm[:], 0.0)
-        nc.vector.memset(e_rows[:], 0.0)
-        for quad in range(4):
-            nc.gpsimd.dma_start(
-                out=b_plane_raw[32 * quad : 32 * quad + 4, :].bitcast(I32),
-                in_=b_scales[0, 4 * quad : 4 * quad + 4, :].bitcast(I32),
-            )
-        make_identity(nc, ident[:])
-
-        def load_a(c):
+        def load_a(engine, c):
             cols = slice(2 * CHUNK * c, 2 * CHUNK * (c + 1))
-            nc.sync.dma_start(out=a_codes[:, cols].bitcast(I32), in_=a_words[0][:, cols].bitcast(I32))
+            engine.dma_start(out=a_codes[:, cols].bitcast(I32), in_=a_words[0][:, cols].bitcast(I32))
 
-        def load_a_scales(quads):
-            for quad in quads:
+        def load_scales(plane, scales):
+            for quad in range(4):
                 nc.sync.dma_start(
-                    out=a_plane[32 * quad : 32 * quad + 4, :].bitcast(I32),
-                    in_=a_scales[0, 4 * quad : 4 * quad + 4, :].bitcast(I32),
+                    out=plane[32 * quad : 32 * quad + 4, :].bitcast(I32),
+                    in_=scales[0, 4 * quad : 4 * quad + 4, :].bitcast(I32),
                 )
 
         def load_r(g, half):
@@ -89,20 +84,26 @@ def tile_ridge_cook_distances_s4_kernel(tc, a_words, a_scales, b_words, b_scales
             for t in range(PACK):
                 nc.sync.dma_start(out=r_raw[:, g, t, cols], in_=rows[t][:, :, cols])
 
-        nc.sync.dma_start(out=b_raw[:].bitcast(I32), in_=b_words[0].bitcast(I32))
-        load_a(0)
-        load_a_scales((0, 1))
-        load_r(0, 0)
-        load_a_scales((2, 3))
+        nc.gpsimd.dma_start(out=b_raw[:].bitcast(I32), in_=b_words[0].bitcast(I32))
+        load_a(nc.gpsimd, 0)
+        nc.vector.memset(b_plane_raw[:].bitcast(I32), 0)
+        nc.vector.memset(a_plane[:].bitcast(I32), 0)
+        nc.vector.memset(vec_rows[:], 0.0)
+        nc.vector.memset(warm[:], 0.0)
+        nc.vector.memset(e_rows[:], 0.0)
+        load_scales(b_plane_raw, b_scales)
+        load_scales(a_plane, a_scales)
         nc.sync.dma_start(out=vec_rows[0:4, :], in_=mu[0:512].rearrange("(q t i) -> t q i", q=16, t=4))
         nc.sync.dma_start(out=vec_rows[4:8, :], in_=mu[512:1024].rearrange("(q t i) -> t q i", q=16, t=4))
+        load_r(0, 0)
         load_r(0, 1)
-        load_a(1)
+        load_a(nc.sync, 1)
         load_r(1, 0)
         load_r(1, 1)
-        load_a(2)
-        load_a(3)
+        load_a(nc.sync, 2)
+        load_a(nc.sync, 3)
         nc.sync.dma_start(out=e_rows[0:TILES, :], in_=e.rearrange("(t p) -> t p", p=LANES))
+        make_identity(nc, ident[:])
         make_identity(nc, ident_f[:])
         nc.gpsimd.memset(d_cols[:], 0.0)
         nc.scalar.activation(out=warm[:], in_=warm[:], func=SQUARE)
@@ -189,13 +190,9 @@ def tile_ridge_cook_distances_s4_kernel(tc, a_words, a_scales, b_words, b_scales
             return [(x_rows[c, g][:, :, cols], x_codes[:, c, g, cols], x_plane[:, c, g, cols], 256) for g in range(GROUPS)]
 
         z2 = {}
-        sums = {}
 
         def stage2(tiles):
-            sum0 = ring.tile([LANES, len(tiles)], F32, tag="sum0", name="sum0")
-            sum1 = ring.tile([LANES, len(tiles)], F32, tag="sum1", name="sum1")
-            sums[tiles[0]] = (sum0, sum1)
-            for j, tile in enumerate(tiles):
+            for tile in tiles:
                 c, lo = tile // 4, LANES * (tile % 4)
                 square = outs.tile([LANES, P], F32, tag="square", name="square")
                 z2[tile] = square
@@ -213,43 +210,42 @@ def tile_ridge_cook_distances_s4_kernel(tc, a_words, a_scales, b_words, b_scales
                             stop=(g == GROUPS - 1),
                         )
                     nc.scalar.activation(
-                        out=square[:, cols], in_=bank[:], func=SQUARE, accum_out=total[:, j : j + 1]
+                        out=square[:, cols], in_=bank[:], func=SQUARE, accum_out=total[:, tile : tile + 1]
                     )
 
         def finish(tiles):
-            n = len(tiles)
-            sum0, sum1 = sums[tiles[0]]
-            rest = ring.tile([LANES, n], F32, tag="rest", name="rest")
-            inv = ring.tile([LANES, n], F32, tag="inv", name="inv")
-            loo = ring.tile([LANES, n], F32, tag="loo", name="loo")
-            both = ring.tile([LANES, n], F32, tag="both", name="both")
-            d_half = ring.tile([LANES, n], F32, tag="d_half", name="d_half")
+            cols = slice(tiles[0], tiles[-1] + 1)
+            last = tiles[-1] == TILES - 1
 
             def small1():
                 nc.vector.scalar_tensor_tensor(
-                    out=rest[:], in0=sum0[:], scalar=-1.0 * P, in1=sum1[:], op0=ADD, op1=ADD
+                    out=rest[:, cols], in0=sum0[:, cols], scalar=-1.0 * P, in1=sum1[:, cols], op0=ADD, op1=ADD
                 )
-                nc.gpsimd.tensor_tensor(out=both[:], in0=sum0[:], in1=sum1[:], op=ADD)
 
             def small2():
-                nc.vector.reciprocal(out=inv[:], in_=rest[:])
+                nc.vector.reciprocal(out=inv[:, cols], in_=rest[:, cols])
+                if last:
+                    nc.vector.tensor_tensor(out=both[:], in0=sum0[:], in1=sum1[:], op=ADD)
 
             def small3():
-                nc.vector.tensor_tensor(out=loo[:], in0=e_col[:, tiles[0] : tiles[0] + n], in1=inv[:], op=MULT)
-                nc.gpsimd.tensor_tensor(out=d_half[:], in0=both[:], in1=loo[:], op=MULT)
-                nc.gpsimd.tensor_tensor(
-                    out=d_cols[:, tiles[0] : tiles[0] + n], in0=d_half[:], in1=loo[:], op=MULT
-                )
+                nc.vector.tensor_tensor(out=loo[:, cols], in0=e_col[:, cols], in1=inv[:, cols], op=MULT)
 
-            def scale(j):
+            def scale(tile):
                 result = outs.tile([LANES, P], F32, tag="result", name="result")
-                nc.vector.tensor_scalar(
-                    out=result[:], in0=z2[tiles[j]][:], scalar1=loo[:, j : j + 1], scalar2=loo[:, j : j + 1],
-                    op0=MULT, op1=MULT,
-                )
-                nc.sync.dma_start(out=out_0[LANES * tiles[j] : LANES * (tiles[j] + 1), :], in_=result[:])
+                pieces = 2 if last else 1
+                for piece in range(pieces):
+                    part = slice(P // pieces * piece, P // pieces * (piece + 1))
+                    nc.vector.tensor_scalar(
+                        out=result[:, part], in0=z2[tile][:, part],
+                        scalar1=loo[:, tile : tile + 1], scalar2=loo[:, tile : tile + 1], op0=MULT, op1=MULT,
+                    )
+                    if last:
+                        nc.vector.tensor_tensor(
+                            out=(d_half[:], d_cols[:, 0:TILES])[piece], in0=(both[:], d_half[:])[piece], in1=loo[:], op=MULT
+                        )
+                    nc.sync.dma_start(out=out_0[LANES * tile : LANES * (tile + 1), part], in_=result[:, part])
 
-            return [small1, small2, small3], [lambda j=j: scale(j) for j in range(n)]
+            return [small1, small2, small3], [lambda tile=tile: scale(tile) for tile in tiles]
 
         def turn_e():
             e_bank = psum.tile([LANES, LANES], BF16, tag="x")

@@ -26,8 +26,9 @@ CHUNK = 512
 CHUNKS = M // CHUNK
 TILES = M // LANES
 GROUPS_OF_TILES = [[2 * i, 2 * i + 1] for i in range(7)] + [[14], [15]]
-ON_VECTOR = {0: (1, 3), 3: (3,)}
-ORDER = "B A00 A01 A10 A11 A20 R0 R1 A21 R2 R3 R4 R5 X0 R6 R7 X1 E X2 P0 X3 G0 P1 P2 P3 X4 G1 G2 A30 A31 P4 G3 X5 X6 P5 P6 G4 X7 P7 P8 G5 G6 G7 G8"
+WARM = 7
+ON_VECTOR = {0: (0, 2, 7), 3: (4,)}
+ORDER = "B A00 R0 R1 A01 A10 X0 A11 A20 R2 R3 R4 R5 R6 R7 A21 E X1 X2 P0 P1 X3 P2 P3 G0 G1 A30 X4 G2 G3 X5 P4 A31 P5 X6 G4 P6 X7 P7 P8 G5 G6 G7 G8"
 
 
 def tile_ridge_cook_distances_s4_kernel(tc, a_words, a_scales, b_words, b_scales, mu, r, e, out_0, out_1):
@@ -84,13 +85,15 @@ def tile_ridge_cook_distances_s4_kernel(tc, a_words, a_scales, b_words, b_scales
             for t in range(PACK):
                 nc.sync.dma_start(out=r_raw[:, g, t, cols], in_=rows[t][:, :, cols])
 
-        nc.gpsimd.dma_start(out=b_raw[:].bitcast(I32), in_=b_words[0].bitcast(I32))
-        load_a(nc.gpsimd, 0)
         nc.vector.memset(b_plane_raw[:].bitcast(I32), 0)
         nc.vector.memset(a_plane[:].bitcast(I32), 0)
         nc.vector.memset(vec_rows[:], 0.0)
+        zeros = keep.tile([LANES, 512], BF16)
+        nc.vector.memset(zeros[:], 0.0)
         nc.vector.memset(warm[:], 0.0)
         nc.vector.memset(e_rows[:], 0.0)
+        nc.gpsimd.dma_start(out=b_raw[:].bitcast(I32), in_=b_words[0].bitcast(I32))
+        load_a(nc.gpsimd, 0)
         load_scales(b_plane_raw, b_scales)
         load_scales(a_plane, a_scales)
         nc.sync.dma_start(out=vec_rows[0:4, :], in_=mu[0:512].rearrange("(q t i) -> t q i", q=16, t=4))
@@ -107,6 +110,10 @@ def tile_ridge_cook_distances_s4_kernel(tc, a_words, a_scales, b_words, b_scales
         make_identity(nc, ident_f[:])
         nc.gpsimd.memset(d_cols[:], 0.0)
         nc.scalar.activation(out=warm[:], in_=warm[:], func=SQUARE)
+
+        warm_bank = psum.tile([LANES, 512], F32, tag="z")
+        for i in range(WARM):
+            nc.tensor.matmul(warm_bank[:], lhsT=zeros[:, 0:LANES], rhs=zeros[:], start=True, stop=True)
 
         def ready_b():
             for g in range(GROUPS):
@@ -276,7 +283,7 @@ def tile_ridge_cook_distances_s4_kernel(tc, a_words, a_scales, b_words, b_scales
                     add_long(lambda i=i, number=number: x_steps(number, i))
             else:
                 for i in range(3):
-                    steps[longs[i - 3]].append(lambda i=i, number=number: short(number, i))
+                    steps[longs[i - (4 if number < 6 else 3)]].append(lambda i=i, number=number: short(number, i))
                 for j in range(len(GROUPS_OF_TILES[number])):
                     add_long(lambda j=j, number=number: scaling(number, j))
 

@@ -26,7 +26,7 @@ CHUNK = 512
 CHUNKS = M // CHUNK
 TILES = M // LANES
 GROUPS_OF_TILES = [[2 * i, 2 * i + 1] for i in range(7)] + [[14], [15]]
-WARM = 7
+WARM = 5
 ON_VECTOR = {0: (0, 2, 7), 3: (4,)}
 ORDER = "B A00 R0 R1 A01 A10 X0 A11 A20 R2 R3 R4 R5 R6 R7 A21 E X1 X2 P0 P1 X3 P2 P3 G0 G1 A30 X4 G2 G3 X5 P4 A31 P5 X6 G4 P6 X7 P7 P8 G5 G6 G7 G8"
 
@@ -68,8 +68,8 @@ def tile_ridge_cook_distances_s4_kernel(tc, a_words, a_scales, b_words, b_scales
         both = keep.tile([LANES, TILES], F32)
         d_half = keep.tile([LANES, TILES], F32)
 
-        def load_a(engine, c):
-            cols = slice(2 * CHUNK * c, 2 * CHUNK * (c + 1))
+        def load_a(engine, first, last):
+            cols = slice(2 * CHUNK * first, 2 * CHUNK * last)
             engine.dma_start(out=a_codes[:, cols].bitcast(I32), in_=a_words[0][:, cols].bitcast(I32))
 
         def load_scales(plane, scales):
@@ -79,32 +79,29 @@ def tile_ridge_cook_distances_s4_kernel(tc, a_words, a_scales, b_words, b_scales
                     in_=scales[0, 4 * quad : 4 * quad + 4, :].bitcast(I32),
                 )
 
-        def load_r(g, half):
+        def load_r(g, cols):
             rows = r[512 * g : 512 * (g + 1), :].rearrange("(q t i) c -> t q i c", q=16, t=4)
-            cols = slice(512 * half, 512 * (half + 1))
             for t in range(PACK):
                 nc.sync.dma_start(out=r_raw[:, g, t, cols], in_=rows[t][:, :, cols])
 
         nc.vector.memset(b_plane_raw[:].bitcast(I32), 0)
-        nc.vector.memset(a_plane[:].bitcast(I32), 0)
         nc.vector.memset(vec_rows[:], 0.0)
+        nc.vector.memset(a_plane[:].bitcast(I32), 0)
         zeros = keep.tile([LANES, 512], BF16)
         nc.vector.memset(zeros[:], 0.0)
         nc.vector.memset(warm[:], 0.0)
         nc.vector.memset(e_rows[:], 0.0)
         nc.gpsimd.dma_start(out=b_raw[:].bitcast(I32), in_=b_words[0].bitcast(I32))
-        load_a(nc.gpsimd, 0)
+        load_a(nc.gpsimd, 0, 1)
         load_scales(b_plane_raw, b_scales)
-        load_scales(a_plane, a_scales)
         nc.sync.dma_start(out=vec_rows[0:4, :], in_=mu[0:512].rearrange("(q t i) -> t q i", q=16, t=4))
         nc.sync.dma_start(out=vec_rows[4:8, :], in_=mu[512:1024].rearrange("(q t i) -> t q i", q=16, t=4))
-        load_r(0, 0)
-        load_r(0, 1)
-        load_a(nc.sync, 1)
-        load_r(1, 0)
-        load_r(1, 1)
-        load_a(nc.sync, 2)
-        load_a(nc.sync, 3)
+        load_scales(a_plane, a_scales)
+        load_r(0, slice(0, 512))
+        load_r(0, slice(512, P))
+        load_a(nc.sync, 1, 2)
+        load_r(1, slice(0, P))
+        load_a(nc.sync, 2, 4)
         nc.sync.dma_start(out=e_rows[0:TILES, :], in_=e.rearrange("(t p) -> t p", p=LANES))
         make_identity(nc, ident[:])
         make_identity(nc, ident_f[:])
@@ -116,19 +113,21 @@ def tile_ridge_cook_distances_s4_kernel(tc, a_words, a_scales, b_words, b_scales
             nc.tensor.matmul(warm_bank[:], lhsT=zeros[:, 0:LANES], rhs=zeros[:], start=True, stop=True)
 
         def ready_b():
-            for g in range(GROUPS):
-                nc.vector.tensor_copy(
-                    out=b_plane[:, 512 * g : 512 * (g + 1)].bitcast(I32).rearrange("p (t q w) -> p t q w", t=4, q=16),
-                    in_=b_plane_raw[:, 512 * g : 512 * (g + 1)].bitcast(I32).rearrange("p (q t w) -> p t q w", t=4, q=16),
-                )
-                nc.vector.tensor_copy(
-                    out=b_codes[:, 1024 * g : 1024 * (g + 1)].bitcast(I32).rearrange("p (t q w) -> p t q w", t=4, q=16),
-                    in_=b_raw[:, 1024 * g : 1024 * (g + 1)].bitcast(I32).rearrange("p (q t w) -> p t q w", t=4, q=16),
-                )
-
+            order_b(0)
             vec_bank = psum.tile([LANES, LANES], BF16, tag="x")
             nc.tensor.transpose(vec_bank[:], vec_rows[:], ident[:])
-            nc.vector.tensor_scalar(out=neg_mu[:], in0=vec_bank[:, 0 : GROUPS * PACK], scalar1=-1.0, scalar2=None, op0=MULT)
+            nc.vector.tensor_scalar(
+                out=neg_mu[:], in0=vec_bank[:, 0 : GROUPS * PACK], scalar1=-1.0, scalar2=None, op0=MULT
+            )
+            order_b(1)
+
+        def order_b(g):
+            for tile, raw, width in ((b_plane, b_plane_raw, 512), (b_codes, b_raw, 1024)):
+                cols = slice(width * g, width * (g + 1))
+                nc.vector.tensor_copy(
+                    out=tile[:, cols].bitcast(I32).rearrange("p (t q w) -> p t q w", t=4, q=16),
+                    in_=raw[:, cols].bitcast(I32).rearrange("p (q t w) -> p t q w", t=4, q=16),
+                )
 
         x_rows = {}
 

from contextlib import ExitStack

import concourse.mybir as mybir
from concourse.masks import make_identity

M, K, P = 2048, 512, 1024
FLOPS = 2 * M * K * P + 2 * M * P * P

F32 = mybir.dt.float32
BF16 = mybir.dt.bfloat16
U32 = mybir.dt.uint32
I32 = mybir.dt.int32
U8 = mybir.dt.uint8
FP8X4 = mybir.dt.float8_e4m3fn_x4
FP4X4 = mybir.dt.float4_e2m1fn_x4
MULT = mybir.AluOpType.mult
ADD = mybir.AluOpType.add
IDENTITY = mybir.ActivationFunctionType.Identity
SQUARE = mybir.ActivationFunctionType.Square
COPY = mybir.ActivationFunctionType.Copy

LANES = 128
PACK = 4
GROUPS = P // 512
CHUNK = 512
CHUNKS = M // CHUNK
TILES = M // LANES
GROUPS_OF_TILES = [[2 * i, 2 * i + 1] for i in range(7)] + [[14], [15]]
WARM = 5
ON_VECTOR = {0: (0, 2, 7), 3: (4,)}
ORDER = "B A00 R0 R1 A01 A10 X0 A11 A20 R2 R3 R4 R5 R6 R7 A21 E X1 X2 P0 P1 X3 P2 P3 G0 G1 A30 X4 G2 G3 X5 P4 A31 P5 X6 G4 P6 X7 P7 P8 G5 G6 G7 G8"


def tile_ridge_cook_distances_s4_kernel(tc, a_words, a_scales, b_words, b_scales, mu, r, e, out_0, out_1):
    nc = tc.nc
    with ExitStack() as ctx:
        keep = ctx.enter_context(tc.tile_pool(name="keep", bufs=1))
        ring = ctx.enter_context(tc.tile_pool(name="ring", bufs=4))
        rows_pool = ctx.enter_context(tc.tile_pool(name="rows", bufs=8))
        outs = ctx.enter_context(tc.tile_pool(name="outs", bufs=8))
        psum = ctx.enter_context(tc.psum_pool(name="psum", bufs=4))
        ctx.enter_context(tc.manual_schedule())

        vec_rows = keep.tile([LANES, LANES], BF16)
        e_rows = keep.tile([LANES, LANES], BF16)
        b_plane_raw = keep.tile([LANES, P], U8, align_bytes=64)
        a_plane = keep.tile([LANES, M], U8, align_bytes=64)
        b_raw = keep.tile([LANES, 2 * P], U8, align_bytes=64)
        b_codes = keep.tile([LANES, 2 * P], U8, align_bytes=64)
        b_plane = keep.tile([LANES, P], U8, align_bytes=64)
        a_codes = keep.tile([LANES, 2 * M], U8, align_bytes=64)
        r_raw = keep.tile([LANES, GROUPS, PACK, P], BF16, align_bytes=64)
        r_codes = keep.tile([LANES, GROUPS, P], U32, align_bytes=64)
        r_plane = keep.tile([LANES, GROUPS, P], U8, align_bytes=64)
        x_codes = keep.tile([LANES, CHUNKS, GROUPS, CHUNK], U32, align_bytes=64)
        x_plane = keep.tile([LANES, CHUNKS, GROUPS, CHUNK], U8, align_bytes=64)
        neg_mu = keep.tile([LANES, GROUPS * PACK], F32)
        e_col = keep.tile([LANES, TILES], F32)
        d_cols = keep.tile([LANES, LANES], F32)
        ident = keep.tile([LANES, LANES], BF16)
        ident_f = keep.tile([LANES, LANES], F32)
        warm = keep.tile([LANES, 1], F32)
        sum0 = keep.tile([LANES, TILES], F32)
        sum1 = keep.tile([LANES, TILES], F32)
        rest = keep.tile([LANES, TILES], F32)
        inv = keep.tile([LANES, TILES], F32)
        loo = keep.tile([LANES, TILES], F32)
        both = keep.tile([LANES, TILES], F32)
        d_half = keep.tile([LANES, TILES], F32)

        def load_a(engine, first, last):
            cols = slice(2 * CHUNK * first, 2 * CHUNK * last)
            engine.dma_start(out=a_codes[:, cols].bitcast(I32), in_=a_words[0][:, cols].bitcast(I32))

        def load_scales(plane, scales):
            for quad in range(4):
                nc.sync.dma_start(
                    out=plane[32 * quad : 32 * quad + 4, :].bitcast(I32),
                    in_=scales[0, 4 * quad : 4 * quad + 4, :].bitcast(I32),
                )

        def load_r(g, cols):
            rows = r[512 * g : 512 * (g + 1), :].rearrange("(q t i) c -> t q i c", q=16, t=4)
            for t in range(PACK):
                nc.sync.dma_start(out=r_raw[:, g, t, cols], in_=rows[t][:, :, cols])

        nc.vector.memset(b_plane_raw[:].bitcast(I32), 0)
        nc.vector.memset(vec_rows[:], 0.0)
        nc.vector.memset(a_plane[:].bitcast(I32), 0)
        zeros = keep.tile([LANES, 512], BF16)
        nc.vector.memset(zeros[:], 0.0)
        nc.vector.memset(warm[:], 0.0)
        nc.vector.memset(e_rows[:], 0.0)
        nc.gpsimd.dma_start(out=b_raw[:].bitcast(I32), in_=b_words[0].bitcast(I32))
        load_a(nc.gpsimd, 0, 1)
        load_scales(b_plane_raw, b_scales)
        nc.sync.dma_start(out=vec_rows[0:4, :], in_=mu[0:512].rearrange("(q t i) -> t q i", q=16, t=4))
        nc.sync.dma_start(out=vec_rows[4:8, :], in_=mu[512:1024].rearrange("(q t i) -> t q i", q=16, t=4))
        load_scales(a_plane, a_scales)
        load_r(0, slice(0, 512))
        load_r(0, slice(512, P))
        load_a(nc.sync, 1, 2)
        load_r(1, slice(0, P))
        load_a(nc.sync, 2, 4)
        nc.sync.dma_start(out=e_rows[0:TILES, :], in_=e.rearrange("(t p) -> t p", p=LANES))
        make_identity(nc, ident[:])
        make_identity(nc, ident_f[:])
        nc.gpsimd.memset(d_cols[:], 0.0)
        nc.scalar.activation(out=warm[:], in_=warm[:], func=SQUARE)

        warm_bank = psum.tile([LANES, 512], F32, tag="z")
        for i in range(WARM):
            nc.tensor.matmul(warm_bank[:], lhsT=zeros[:, 0:LANES], rhs=zeros[:], start=True, stop=True)

        def ready_b():
            order_b(0)
            vec_bank = psum.tile([LANES, LANES], BF16, tag="x")
            nc.tensor.transpose(vec_bank[:], vec_rows[:], ident[:])
            nc.vector.tensor_scalar(
                out=neg_mu[:], in0=vec_bank[:, 0 : GROUPS * PACK], scalar1=-1.0, scalar2=None, op0=MULT
            )
            order_b(1)

        def order_b(g):
            for tile, raw, width in ((b_plane, b_plane_raw, 512), (b_codes, b_raw, 1024)):
                cols = slice(width * g, width * (g + 1))
                nc.vector.tensor_copy(
                    out=tile[:, cols].bitcast(I32).rearrange("p (t q w) -> p t q w", t=4, q=16),
                    in_=raw[:, cols].bitcast(I32).rearrange("p (q t w) -> p t q w", t=4, q=16),
                )

        x_rows = {}

        def stage1(c, g, on_vector):
            cols = slice(CHUNK * c, CHUNK * (c + 1))
            if True:
                rows = rows_pool.tile([LANES, PACK, CHUNK], BF16, tag="rows", name=f"rows_{c}_{g}")
                x_rows[c, g] = rows
                for t in range(PACK):
                    s = PACK * g + t
                    bank = psum.tile([LANES, CHUNK], F32, tag="x")
                    nc.tensor.matmul_mx(
                        out=bank[:],
                        lhsT=b_codes[:, 256 * s : 256 * (s + 1)].bitcast(FP4X4),
                        lhsT_scale=b_plane[:, LANES * s : LANES * (s + 1)],
                        rhs=a_codes[:, 2 * CHUNK * c : 2 * CHUNK * (c + 1)].bitcast(FP4X4),
                        rhs_scale=a_plane[:, cols],
                        start=True,
                        stop=True,
                    )
                    if s in on_vector:
                        nc.vector.tensor_scalar(
                            out=rows[:, t, :], in0=bank[:], scalar1=neg_mu[:, s : s + 1], scalar2=None, op0=ADD
                        )
                    else:
                        nc.scalar.activation(out=rows[:, t, :], in_=bank[:], func=IDENTITY, bias=neg_mu[:, s : s + 1])

        def interleave(rows, width):
            grouped = ring.tile([LANES, width, PACK], BF16, tag=f"grouped{width}", align_bytes=64, name="grouped")
            nc.vector.tensor_copy(
                out=grouped[:].rearrange("p (c i) t -> p c t i", i=4),
                in_=rows.rearrange("p t (c i) -> p c t i", i=4),
            )
            return grouped

        def quantize(grouped, codes, plane):
            nc.vector.quantize_mx(
                out=codes.bitcast(FP8X4), scales=plane, in_=grouped[:].rearrange("p c t -> p (c t)")
            )

        def quantize_steps(units):
            made = {}
            steps = []

            def inter(i):
                made[i] = interleave(units[i][0], units[i][3])

            def quant(i):
                quantize(made[i], units[i][1], units[i][2])

            for i in range(0, len(units), 2):
                steps += [lambda i=i: inter(i), lambda i=i: inter(i + 1)]
                steps += [lambda i=i: quant(i), lambda i=i: quant(i + 1)]
            return steps

        def r_units():
            units = []
            for g in range(GROUPS):
                for half in range(2):
                    cols = slice(512 * half, 512 * (half + 1))
                    units.append((r_raw[:, g, :, cols], r_codes[:, g, cols], r_plane[:, g, cols], 512))
            return units

        def x_units(pair):
            c, cols = pair // 2, slice(256 * (pair % 2), 256 * (pair % 2 + 1))
            return [(x_rows[c, g][:, :, cols], x_codes[:, c, g, cols], x_plane[:, c, g, cols], 256) for g in range(GROUPS)]

        z2 = {}

        def stage2(tiles):
            for tile in tiles:
                c, lo = tile // 4, LANES * (tile % 4)
                square = outs.tile([LANES, P], F32, tag="square", name="square")
                z2[tile] = square
                for half, total in ((0, sum0), (1, sum1)):
                    cols = slice(512 * half, 512 * (half + 1))
                    bank = psum.tile([LANES, 512], F32, tag="z")
                    for g in range(GROUPS):
                        nc.tensor.matmul_mx(
                            out=bank[:],
                            lhsT=x_codes[:, c, g, lo : lo + LANES].bitcast(FP8X4),
                            lhsT_scale=x_plane[:, c, g, lo : lo + LANES],
                            rhs=r_codes[:, g, cols].bitcast(FP8X4),
                            rhs_scale=r_plane[:, g, cols],
                            start=(g == 0),
                            stop=(g == GROUPS - 1),
                        )
                    nc.scalar.activation(
                        out=square[:, cols], in_=bank[:], func=SQUARE, accum_out=total[:, tile : tile + 1]
                    )

        def finish(tiles):
            cols = slice(tiles[0], tiles[-1] + 1)
            last = tiles[-1] == TILES - 1

            def small1():
                nc.vector.scalar_tensor_tensor(
                    out=rest[:, cols], in0=sum0[:, cols], scalar=-1.0 * P, in1=sum1[:, cols], op0=ADD, op1=ADD
                )

            def small2():
                nc.vector.reciprocal(out=inv[:, cols], in_=rest[:, cols])
                if last:
                    nc.vector.tensor_tensor(out=both[:], in0=sum0[:], in1=sum1[:], op=ADD)

            def small3():
                nc.vector.tensor_tensor(out=loo[:, cols], in0=e_col[:, cols], in1=inv[:, cols], op=MULT)

            def scale(tile):
                result = outs.tile([LANES, P], F32, tag="result", name="result")
                pieces = 2 if last else 1
                for piece in range(pieces):
                    part = slice(P // pieces * piece, P // pieces * (piece + 1))
                    nc.vector.tensor_scalar(
                        out=result[:, part], in0=z2[tile][:, part],
                        scalar1=loo[:, tile : tile + 1], scalar2=loo[:, tile : tile + 1], op0=MULT, op1=MULT,
                    )
                    if last:
                        nc.vector.tensor_tensor(
                            out=(d_half[:], d_cols[:, 0:TILES])[piece], in0=(both[:], d_half[:])[piece], in1=loo[:], op=MULT
                        )
                    nc.sync.dma_start(out=out_0[LANES * tile : LANES * (tile + 1), part], in_=result[:, part])

            return [small1, small2, small3], [lambda tile=tile: scale(tile) for tile in tiles]

        def turn_e():
            e_bank = psum.tile([LANES, LANES], BF16, tag="x")
            nc.tensor.transpose(e_bank[:], e_rows[:], ident[:])
            nc.vector.tensor_scalar(out=e_col[:], in0=e_bank[:, 0:TILES], scalar1=-1.0 * P, scalar2=None, op0=MULT)

        steps = []
        longs = []

        def add_long(step):
            longs.append(len(steps))
            steps.append([step])

        for token in ORDER.split(" "):
            kind, number = token[0], int(token[1:] or "0")
            if kind == "A":
                steps.append([lambda number=number: stage1(number // 10, number % 10, ON_VECTOR.get(number // 10, ()))])
            elif kind == "P":
                steps.append([lambda number=number: stage2(GROUPS_OF_TILES[number])])
            elif kind == "E":
                steps.append([turn_e])
            elif kind == "B":
                steps.append([ready_b])
            elif kind == "R":
                add_long(lambda number=number: r_steps(number))
            elif kind == "X":
                for i in range(4):
                    add_long(lambda i=i, number=number: x_steps(number, i))
            else:
                for i in range(3):
                    steps[longs[i - (4 if number < 6 else 3)]].append(lambda i=i, number=number: short(number, i))
                for j in range(len(GROUPS_OF_TILES[number])):
                    add_long(lambda j=j, number=number: scaling(number, j))

        cache = {}

        def r_steps(i):
            if "r" not in cache:
                cache["r"] = quantize_steps(r_units())
            cache["r"][i]()

        def x_steps(c, i):
            if ("x", c) not in cache:
                cache["x", c] = quantize_steps(x_units(c))
            cache["x", c][i]()

        def short(p, i):
            if ("f", p) not in cache:
                cache["f", p] = finish(GROUPS_OF_TILES[p])
            cache["f", p][0][i]()

        def scaling(p, j):
            cache["f", p][1][j]()

        for group in steps:
            for step in group:
                step()

        d_bank = psum.tile([LANES, LANES], F32, tag="x")
        nc.tensor.transpose(d_bank[:], d_cols[:], ident_f[:])
        d_rows = keep.tile([TILES, LANES], F32)
        nc.scalar.activation(out=d_rows[:], in_=d_bank[0:TILES, :], func=COPY, scale=1.0 / P)
        nc.sync.dma_start(out=out_1.rearrange("(t p) -> t p", p=LANES), in_=d_rows[:])
